import numpy as np, ml_dtypes
CORES = [23,119,17,113]
N = 4
TK = 128
def setup_inputs(rng):
    return {"x": rng.standard_normal((N, 128, TK), dtype=np.float32).astype(ml_dtypes.bfloat16), "w": rng.standard_normal((N, 128, 128), dtype=np.float32).astype(ml_dtypes.bfloat16)}
def setup_inputs_big(rng):
    d = setup_inputs(rng)
    for k in ("x", "w"): d[k] = (d[k].astype(np.float32) * 1024.0).astype(d[k].dtype)
    return d
def setup_inputs_small(rng):
    d = setup_inputs(rng)
    for k in ("x", "w"): d[k] = (d[k].astype(np.float32) * (1 / 1024.0)).astype(d[k].dtype)
    return d
def setup_inputs_apart(rng):
    d = setup_inputs(rng)
    f = (10.0 ** rng.permutation(np.linspace(-1.5, 1.5, N))).astype(np.float32).reshape(N, 1, 1)
    for k in ("x", "w"): d[k] = (d[k].astype(np.float32) * f).astype(d[k].dtype)
    return d
def setup_inputs_neg(rng):
    d = setup_inputs(rng)
    d["x"] = (np.abs(d["x"].astype(np.float32)) * 1048576.0).astype(d["x"].dtype); d["w"] = (-np.abs(d["w"].astype(np.float32))).astype(d["w"].dtype)
    return d
def reference(x, w):
    X, W = x.astype(np.float64), w.astype(np.float64)
    y = np.stack([np.max([W[j].T @ X[r] for j in range(N)], axis=0) for r in range(N)])
    return {"y": y.astype(ml_dtypes.bfloat16)}

@@ -1,0 +1,95 @@
+from concourse.bass import DstId, RemoteDMATransfer
+from concourse.mybir import AluOpType
+
+N = 4
+D = 128
+
+SCRATCH = {
+    "xs": ("sbuf", [D, D], "bfloat16"),
+    "ys": ("sbuf", [D, D], "bfloat16"),
+}
+for _j in range(N):
+    SCRATCH["w%d" % _j] = ("sbuf", [D, D], "bfloat16")
+    SCRATCH["p%d" % _j] = ("psum", [D, 512], "float32")
+for _j in range(N - 1):
+    SCRATCH["m%d" % _j] = ("sbuf", [D, D], "float32")
+
+SEMAPHORES = (["wld", "xld", "sent", "stored"]
+              + ["arr%d" % j for j in range(N)]
+              + ["mm%d" % j for j in range(N)]
+              + ["vx%d" % j for j in range(N)])
+
+NEAR_ENGINES = 8
+FAR_ENGINES = 4
+
+
+def _engines(mask):
+    return [b for b in range(mask.bit_length()) if (mask >> b) & 1]
+
+
+def _mask(engines):
+    m = 0
+    for b in engines:
+        m |= 1 << b
+    return m
+
+
+def rank_program(g, core, T, topo):
+    rank = T.rank_of(core)
+    if rank is None:
+        return
+    others = [c for c in T.cores if c != core]
+    near = [c for c in others if topo.chip(c) == topo.chip(core)]
+    far = [c for c in others if topo.chip(c) != topo.chip(core)]
+    for c in others:
+        assert topo.may_write(core, c)
+
+    plan = {}
+    used = []
+    for c in far + near:
+        want = FAR_ENGINES if c in far else NEAR_ENGINES
+        free = [b for b in _engines(topo.mask(core, c)) if b not in used]
+        if c in near:
+            free = free[::-1]
+        plan[c] = free[:want]
+        assert len(plan[c]) == want
+        used += plan[c]
+
+    my_w = T["w%d" % rank]
+
+    g.sync.dma_start(my_w[:], T.w[:]).then_inc(T.sem.wld, 16)
+    g.sync.dma_start(T.xs[:], T.x[:]).then_inc(T.sem.xld, 16)
+
+    g.wait_ge(T.sem.wld, 16)
+    transfers = []
+    for c in far + near:
+        rid, pid, _se = topo.addr(c)
+        transfers.append(RemoteDMATransfer(
+            dst_ids=[DstId(rid=rid, pnc=pid)], dma_engine_mask=_mask(plan[c]),
+            remote_sem=T.sem["arr%d" % rank], src=my_w[:], dst=my_w[:]))
+    g.remote_dma_fused(transfers, local_sem=T.sem.sent)
+    g.wait_ge(T.sem.sent, len(used))
+
+    order = [core] + near + far
+    g.tensor.wait_ge(T.sem.xld, 16)
+    for step, c in enumerate(order):
+        j = T.rank_of(c)
+        if c == core:
+            g.tensor.wait_ge(T.sem.wld, 16)
+        else:
+            g.tensor.wait_ge(T.sem["arr%d" % j], NEAR_ENGINES if c in near else FAR_ENGINES)
+        p = T["p%d" % step]
+        g.tensor.matmul(p[:, 0:D], T["w%d" % j][:], T.xs[:], True, True).then_inc(T.sem["mm%d" % step], 1)
+
+        g.vector.wait_ge(T.sem["mm%d" % step], 1)
+        if step == 0:
+            g.vector.tensor_copy(T.m0[:], p[:, 0:D]).then_inc(T.sem.vx0, 1)
+        else:
+            g.vector.wait_ge(T.sem["vx%d" % (step - 1)], 1)
+            out = T.ys if step == N - 1 else T["m%d" % step]
+            g.vector.tensor_tensor(out[:], T["m%d" % (step - 1)][:], p[:, 0:D], AluOpType.max).then_inc(
+                T.sem["vx%d" % step], 1)
+
+    g.sync.wait_ge(T.sem["vx%d" % (N - 1)], 1)
+    g.sync.dma_start(T.y[:], T.ys[:]).then_inc(T.sem.stored, 16)
+    g.sync.wait_ge(T.sem.stored, 16)

@@ -3,24 +3,28 @@ from concourse.mybir import AluOpType
 
 N = 4
 D = 128
+H = D // 2
+
+PIECES = [[(0, D)]] + [[(0, H), (H, D)] for _s in range(N - 1)]
 
 SCRATCH = {
+    "wd": ("dram", [D, D], "bfloat16"),
     "xs": ("sbuf", [D, D], "bfloat16"),
     "ys": ("sbuf", [D, D], "bfloat16"),
 }
 for _j in range(N):
     SCRATCH["w%d" % _j] = ("sbuf", [D, D], "bfloat16")
-    SCRATCH["p%d" % _j] = ("psum", [D, 512], "float32")
-for _j in range(N - 1):
-    SCRATCH["m%d" % _j] = ("sbuf", [D, D], "float32")
+for _s in range(N):
+    for _k in range(len(PIECES[_s])):
+        SCRATCH["p%d_%d" % (_s, _k)] = ("psum", [D, 512], "float32")
+for _s in range(N - 1):
+    SCRATCH["m%d" % _s] = ("sbuf", [D, D], "float32")
 
-SEMAPHORES = (["wld", "xld", "sent", "stored"]
+SEMAPHORES = (["wld", "xld", "wsl", "sent"]
+              + ["st%d" % k for k in range(len(PIECES[N - 1]))]
               + ["arr%d" % j for j in range(N)]
-              + ["mm%d" % j for j in range(N)]
-              + ["vx%d" % j for j in range(N)])
-
-NEAR_ENGINES = 8
-FAR_ENGINES = 4
+              + ["mm%d_%d" % (s, k) for s in range(N) for k in range(len(PIECES[s]))]
+              + ["vx%d_%d" % (s, k) for s in range(N) for k in range(len(PIECES[s]))])
 
 
 def _engines(mask):
@@ -34,62 +38,76 @@ def _mask(engines):
     return m
 
 
+def _dst(topo, c):
+    rid, pid, _se = topo.addr(c)
+    return DstId(rid=rid, pnc=pid)
+
+
 def rank_program(g, core, T, topo):
     rank = T.rank_of(core)
     if rank is None:
         return
     others = [c for c in T.cores if c != core]
-    near = [c for c in others if topo.chip(c) == topo.chip(core)]
-    far = [c for c in others if topo.chip(c) != topo.chip(core)]
     for c in others:
         assert topo.may_write(core, c)
+    near = [c for c in others if topo.chip(c) == topo.chip(core)]
+    far = sorted([c for c in others if topo.chip(c) != topo.chip(core)],
+                 key=lambda c: topo.die(c) != topo.die(core))
+    assert len(near) == 1 and len(far) == 2
+    assert topo.die(far[0]) == topo.die(core) and topo.die(far[1]) != topo.die(core)
 
-    plan = {}
-    used = []
-    for c in far + near:
-        want = FAR_ENGINES if c in far else NEAR_ENGINES
-        free = [b for b in _engines(topo.mask(core, c)) if b not in used]
-        if c in near:
-            free = free[::-1]
-        plan[c] = free[:want]
-        assert len(plan[c]) == want
-        used += plan[c]
+    far_eng = _engines(topo.mask(core, far[0]) & topo.mask(core, far[1]))
+    near_eng = [b for b in _engines(topo.mask(core, near[0])) if b not in far_eng]
+    n_far, n_near = len(far_eng), len(near_eng)
+    assert D % n_far == 0 and D % n_near == 0
 
     my_w = T["w%d" % rank]
 
-    g.sync.dma_start(my_w[:], T.w[:]).then_inc(T.sem.wld, 16)
-    g.sync.dma_start(T.xs[:], T.x[:]).then_inc(T.sem.xld, 16)
+    g.sync.dma_start(T.wd[:], T.w[:]).then_inc(T.sem.wld, 16)
+    g.scalar.wait_ge(T.sem.wld, 16)
+    g.scalar.dma_start(T.xs[:], T.x[:]).then_inc(T.sem.xld, 16)
+    g.sync.wait_ge(T.sem.wld, 16)
+    g.sync.dma_start(my_w[:], T.w[:]).then_inc(T.sem.wsl, 16)
 
     g.wait_ge(T.sem.wld, 16)
-    transfers = []
-    for c in far + near:
-        rid, pid, _se = topo.addr(c)
-        transfers.append(RemoteDMATransfer(
-            dst_ids=[DstId(rid=rid, pnc=pid)], dma_engine_mask=_mask(plan[c]),
-            remote_sem=T.sem["arr%d" % rank], src=my_w[:], dst=my_w[:]))
-    g.remote_dma_fused(transfers, local_sem=T.sem.sent)
-    g.wait_ge(T.sem.sent, len(used))
+    arr = T.sem["arr%d" % rank]
+    g.remote_dma_fused([
+        RemoteDMATransfer(dst_ids=[_dst(topo, c) for c in far], dma_engine_mask=_mask(far_eng), remote_sem=arr,
+                          srcs=[T.wd[:]], dsts=[my_w[:] for _c in far]),
+        RemoteDMATransfer(dst_ids=[_dst(topo, near[0])], dma_engine_mask=_mask(near_eng), remote_sem=arr,
+                          srcs=[T.wd[:]], dsts=[my_w[:]]),
+    ], local_sem=T.sem.sent)
+    g.wait_ge(T.sem.sent, n_far + n_near)
 
     order = [core] + near + far
     g.tensor.wait_ge(T.sem.xld, 16)
-    for step, c in enumerate(order):
+    for s, c in enumerate(order):
         j = T.rank_of(c)
         if c == core:
-            g.tensor.wait_ge(T.sem.wld, 16)
+            g.tensor.wait_ge(T.sem.wsl, 16)
         else:
-            g.tensor.wait_ge(T.sem["arr%d" % j], NEAR_ENGINES if c in near else FAR_ENGINES)
-        p = T["p%d" % step]
-        g.tensor.matmul(p[:, 0:D], T["w%d" % j][:], T.xs[:], True, True).then_inc(T.sem["mm%d" % step], 1)
+            g.tensor.wait_ge(T.sem["arr%d" % j], n_near if c in near else n_far)
+        for k, (lo, hi) in enumerate(PIECES[s]):
+            p = T["p%d_%d" % (s, k)]
+            g.tensor.matmul(p[:, 0:hi - lo], T["w%d" % j][:], T.xs[:, lo:hi], True, True).then_inc(
+                T.sem["mm%d_%d" % (s, k)], 1)
 
-        g.vector.wait_ge(T.sem["mm%d" % step], 1)
-        if step == 0:
-            g.vector.tensor_copy(T.m0[:], p[:, 0:D]).then_inc(T.sem.vx0, 1)
-        else:
-            g.vector.wait_ge(T.sem["vx%d" % (step - 1)], 1)
-            out = T.ys if step == N - 1 else T["m%d" % step]
-            g.vector.tensor_tensor(out[:], T["m%d" % (step - 1)][:], p[:, 0:D], AluOpType.max).then_inc(
-                T.sem["vx%d" % step], 1)
+            done = T.sem["vx%d_%d" % (s, k)]
+            if s == 0:
+                g.vector.wait_ge(T.sem["mm%d_%d" % (s, k)], 1)
+                g.vector.tensor_copy(T.m0[:, lo:hi], p[:, 0:hi - lo]).then_inc(done, 1)
+                continue
+            for k0, (lo0, hi0) in enumerate(PIECES[s - 1]):
+                if lo0 < hi and lo < hi0:
+                    g.vector.wait_ge(T.sem["vx%d_%d" % (s - 1, k0)], 1)
+            g.vector.wait_ge(T.sem["mm%d_%d" % (s, k)], 1)
+            out = T.ys if s == N - 1 else T["m%d" % s]
+            g.vector.tensor_tensor(out[:, lo:hi], T["m%d" % (s - 1)][:, lo:hi], p[:, 0:hi - lo],
+                                   AluOpType.max).then_inc(done, 1)
 
-    g.sync.wait_ge(T.sem["vx%d" % (N - 1)], 1)
-    g.sync.dma_start(T.y[:], T.ys[:]).then_inc(T.sem.stored, 16)
-    g.sync.wait_ge(T.sem.stored, 16)
+    queues = [g.scalar, g.sync]
+    for k, (lo, hi) in enumerate(PIECES[N - 1]):
+        q = queues[k % len(queues)]
+        q.wait_ge(T.sem["vx%d_%d" % (N - 1, k)], 1)
+        q.dma_start(T.y[:, lo:hi], T.ys[:, lo:hi]).then_inc(T.sem["st%d" % k], 16)
+        q.wait_ge(T.sem["st%d" % k], 16)

from concourse.bass import DstId, RemoteDMATransfer
from concourse.mybir import AluOpType

N = 4
D = 128
H = D // 2

PIECES = [[(0, D)]] + [[(0, H), (H, D)] for _s in range(N - 1)]

SCRATCH = {
    "wd": ("dram", [D, D], "bfloat16"),
    "xs": ("sbuf", [D, D], "bfloat16"),
    "ys": ("sbuf", [D, D], "bfloat16"),
}
for _j in range(N):
    SCRATCH["w%d" % _j] = ("sbuf", [D, D], "bfloat16")
for _s in range(N):
    for _k in range(len(PIECES[_s])):
        SCRATCH["p%d_%d" % (_s, _k)] = ("psum", [D, 512], "float32")
for _s in range(N - 1):
    SCRATCH["m%d" % _s] = ("sbuf", [D, D], "float32")

SEMAPHORES = (["wld", "xld", "wsl", "sent"]
              + ["st%d" % k for k in range(len(PIECES[N - 1]))]
              + ["arr%d" % j for j in range(N)]
              + ["mm%d_%d" % (s, k) for s in range(N) for k in range(len(PIECES[s]))]
              + ["vx%d_%d" % (s, k) for s in range(N) for k in range(len(PIECES[s]))])


def _engines(mask):
    return [b for b in range(mask.bit_length()) if (mask >> b) & 1]


def _mask(engines):
    m = 0
    for b in engines:
        m |= 1 << b
    return m


def _dst(topo, c):
    rid, pid, _se = topo.addr(c)
    return DstId(rid=rid, pnc=pid)


def rank_program(g, core, T, topo):
    rank = T.rank_of(core)
    if rank is None:
        return
    others = [c for c in T.cores if c != core]
    for c in others:
        assert topo.may_write(core, c)
    near = [c for c in others if topo.chip(c) == topo.chip(core)]
    far = sorted([c for c in others if topo.chip(c) != topo.chip(core)],
                 key=lambda c: topo.die(c) != topo.die(core))
    assert len(near) == 1 and len(far) == 2
    assert topo.die(far[0]) == topo.die(core) and topo.die(far[1]) != topo.die(core)

    far_eng = _engines(topo.mask(core, far[0]) & topo.mask(core, far[1]))
    near_eng = [b for b in _engines(topo.mask(core, near[0])) if b not in far_eng]
    n_far, n_near = len(far_eng), len(near_eng)
    assert D % n_far == 0 and D % n_near == 0

    my_w = T["w%d" % rank]

    g.sync.dma_start(T.wd[:], T.w[:]).then_inc(T.sem.wld, 16)
    g.scalar.wait_ge(T.sem.wld, 16)
    g.scalar.dma_start(T.xs[:], T.x[:]).then_inc(T.sem.xld, 16)
    g.sync.wait_ge(T.sem.wld, 16)
    g.sync.dma_start(my_w[:], T.w[:]).then_inc(T.sem.wsl, 16)

    g.wait_ge(T.sem.wld, 16)
    arr = T.sem["arr%d" % rank]
    g.remote_dma_fused([
        RemoteDMATransfer(dst_ids=[_dst(topo, c) for c in far], dma_engine_mask=_mask(far_eng), remote_sem=arr,
                          srcs=[T.wd[:]], dsts=[my_w[:] for _c in far]),
        RemoteDMATransfer(dst_ids=[_dst(topo, near[0])], dma_engine_mask=_mask(near_eng), remote_sem=arr,
                          srcs=[T.wd[:]], dsts=[my_w[:]]),
    ], local_sem=T.sem.sent)
    g.wait_ge(T.sem.sent, n_far + n_near)

    order = [core] + near + far
    g.tensor.wait_ge(T.sem.xld, 16)
    for s, c in enumerate(order):
        j = T.rank_of(c)
        if c == core:
            g.tensor.wait_ge(T.sem.wsl, 16)
        else:
            g.tensor.wait_ge(T.sem["arr%d" % j], n_near if c in near else n_far)
        for k, (lo, hi) in enumerate(PIECES[s]):
            p = T["p%d_%d" % (s, k)]
            g.tensor.matmul(p[:, 0:hi - lo], T["w%d" % j][:], T.xs[:, lo:hi], True, True).then_inc(
                T.sem["mm%d_%d" % (s, k)], 1)

            done = T.sem["vx%d_%d" % (s, k)]
            if s == 0:
                g.vector.wait_ge(T.sem["mm%d_%d" % (s, k)], 1)
                g.vector.tensor_copy(T.m0[:, lo:hi], p[:, 0:hi - lo]).then_inc(done, 1)
                continue
            for k0, (lo0, hi0) in enumerate(PIECES[s - 1]):
                if lo0 < hi and lo < hi0:
                    g.vector.wait_ge(T.sem["vx%d_%d" % (s - 1, k0)], 1)
            g.vector.wait_ge(T.sem["mm%d_%d" % (s, k)], 1)
            out = T.ys if s == N - 1 else T["m%d" % s]
            g.vector.tensor_tensor(out[:, lo:hi], T["m%d" % (s - 1)][:, lo:hi], p[:, 0:hi - lo],
                                   AluOpType.max).then_inc(done, 1)

    queues = [g.scalar, g.sync]
    for k, (lo, hi) in enumerate(PIECES[N - 1]):
        q = queues[k % len(queues)]
        q.wait_ge(T.sem["vx%d_%d" % (N - 1, k)], 1)
        q.dma_start(T.y[:, lo:hi], T.ys[:, lo:hi]).then_inc(T.sem["st%d" % k], 16)
        q.wait_ge(T.sem["st%d" % k], 16)
